import numpy as np
import ml_dtypes


def mxq(x, axis, fmt="e4m3"):
    dtype, down = {"e4m3": (ml_dtypes.float8_e4m3fn, 7), "e5m2": (ml_dtypes.float8_e5m2, 14)}[fmt]
    v = np.moveaxis(np.asarray(x, np.float32).astype(ml_dtypes.bfloat16).astype(np.float64), axis, -1)
    blocks = v.reshape(v.shape[:-1] + (-1, 32))
    amax = np.abs(blocks).max(-1, keepdims=True)
    byte = np.maximum(np.where(amax > 0, np.frexp(amax)[1] - 1 + 127, 0) - down, 1)
    scale = np.exp2(byte - 127.0)
    codes = (blocks / scale).astype(np.float32).astype(dtype).astype(np.float64)
    return np.moveaxis((codes * scale).reshape(v.shape), -1, axis)


WIDE = False


def mx_kscale(k):
    if not WIDE:
        return np.ones(k)
    levels = np.array([10, -10, 5, -5, 0])
    if k % 512:
        return np.exp2(np.random.permutation(np.resize(levels, k // 32))).repeat(32)
    a = np.empty((k // 512, 16))
    for p in range(k // 512):
        a[p, :8] = np.random.permutation(np.resize(levels, 8))
        for g in range(8):
            far = levels[np.abs(levels - a[p, g]) >= 10]
            a[p, g + 8] = far[np.random.randint(len(far))]
    return np.exp2(a.ravel()).repeat(32)


def f64(x):
    return np.asarray(x).astype(np.float64)


def striped(idx):
    return np.tile(idx.reshape(-1, 16).T, (8, 1)).astype(np.uint16)


def unstriped(offs):
    return offs[:16].T.reshape(-1).astype(np.int64)


E2M1 = np.array([0.0, 0.5, 1.0, 1.5, 2.0, 3.0, 4.0, 6.0, -0.0, -0.5, -1.0, -1.5, -2.0, -3.0, -4.0, -6.0])


def pack_weight(w, fmt):
    k, n = w.shape
    w = f64(np.asarray(w, np.float32).astype(ml_dtypes.bfloat16)).reshape(k // 32, 32, n)
    amax = np.abs(w).max(1)
    if fmt == "e4m3":
        byte = np.frexp(amax)[1] - 1 + 127 - 7
    else:
        mant, ex = np.frexp(amax / 6.0)
        byte = np.where(mant > 0.5, ex, ex - 1) + 127
    byte = np.clip(np.where(amax > 0, byte, 1), 1, 254)
    scaled = (w * np.exp2(127.0 - byte)[:, None, :]).reshape(k, n).astype(np.float32)
    by_word = np.ascontiguousarray(scaled.reshape(k // 512, 128, 4, n).transpose(0, 1, 3, 2))
    if fmt == "e4m3":
        words = by_word.astype(ml_dtypes.float8_e4m3fn).view(np.uint8)
    else:
        c = by_word.astype(ml_dtypes.float4_e2m1fn).view(np.uint8) & 0xF
        words = (c[..., 0::2] | (c[..., 1::2] << 4)).reshape(k // 512, 128, 2 * n)
    return np.ascontiguousarray(words), np.ascontiguousarray(byte.astype(np.uint8).reshape(k // 512, 16, n))


def unpack_weight(words, scales, fmt):
    g, _, n = scales.shape
    words = np.ascontiguousarray(words).reshape(g, 128, n, -1)
    if fmt == "e4m3":
        vals = words.view(ml_dtypes.float8_e4m3fn).astype(np.float64)
    else:
        nib = np.empty((g, 128, n, 4), np.uint8)
        nib[..., 0::2] = words & 0xF
        nib[..., 1::2] = words >> 4
        vals = E2M1[nib]
    vals = vals * np.repeat(np.exp2(scales.astype(np.float64) - 127.0), 8, axis=1)[..., None]
    return vals.transpose(0, 1, 3, 2).reshape(g * 512, n)


def silu(v):
    return v / (1.0 + np.exp(-np.maximum(v, -700.0)))


K, M, T, S = 1536, 512, 2048, 1024


def setup_inputs():
    n = np.random.standard_normal
    s = mx_kscale(K)[:, None]
    u = mx_kscale(512)[:, None]
    v = pack_weight(n((K, T)) * s, "e4m3")
    p_w2 = pack_weight(1.4 * n((512, M)) / np.sqrt(512) / u, "e2m1")
    return {
        "tab_words": v[0],
        "tab_scales": v[1],
        "w1": (n((K, 512)) / np.sqrt(K) / s * u.T).astype(np.float32),
        "w2_words": p_w2[0],
        "w2_scales": p_w2[1],
        "gT": n((M, T)).astype(np.float32),
        "b": (0.3 * n(512)).astype(np.float32),
        "offs": striped(np.random.permutation(T)[:S]),
    }


def reference(tab_words, tab_scales, w1, w2_words, w2_scales, gT, b, offs):
    tab_ = unpack_weight(tab_words, tab_scales, "e4m3")[:, unstriped(offs)]
    w1_ = mxq(f64(w1), 0, "e4m3")
    w2_ = unpack_weight(w2_words, w2_scales, "e2m1")
    h_ = mxq(np.maximum(w1_.T @ tab_, 0.0), 0, "e4m3")
    y = w2_.T @ h_
    return (silu(y + f64(b)[:, None])) * f64(gT)[:, unstriped(offs)]

@@ -1,0 +1,191 @@
+from contextlib import ExitStack
+
+import concourse.mybir as mybir
+
+K, M, T, S, H = 1536, 512, 2048, 1024, 512
+FLOPS = 2 * K * H * S + 2 * H * M * S
+
+F32 = mybir.dt.float32
+BF16 = mybir.dt.bfloat16
+I32 = mybir.dt.int32
+U32 = mybir.dt.uint32
+U16 = mybir.dt.uint16
+U8 = mybir.dt.uint8
+FP8X4 = mybir.dt.float8_e4m3fn_x4
+FP4X4 = mybir.dt.float4_e2m1fn_x4
+ACT = mybir.ActivationFunctionType
+MULT = mybir.AluOpType.mult
+
+P = 128
+PACK = 4
+PASSES = K // (P * PACK)
+BANKS = 8
+HALF = S // 2
+N_TILES = M // P
+
+
+def tile_list_tabgate_silu_kernel(
+    tc, tab_words, tab_scales, w1, w2_words, w2_scales, gT, b, offs, out
+):
+    nc = tc.nc
+    with ExitStack() as ctx:
+        keep = ctx.enter_context(tc.tile_pool(name="keep", bufs=1))
+        psum = ctx.enter_context(tc.psum_pool(name="psum", bufs=1))
+
+        def entries(j0, j1):
+            return offsets[:, j0 // 16 : j1 // 16]
+
+        offsets = keep.tile([P, S // 16], U16, name="offsets")
+        nc.sync.dma_start(offsets[:], offs)
+
+        warm = keep.tile([P, 8], F32, name="warm")
+        warm_out = keep.tile([P, 8], F32, name="warm_out")
+        nc.vector.memset(warm[:], 0.0)
+        nc.scalar.activation(warm_out[:], warm[:], ACT.Silu)
+
+        tab_plane = keep.tile([P, T], U8, name="tab_plane", align_bytes=64)
+        w2_plane = keep.tile([P, M], U8, name="w2_plane", align_bytes=64)
+        nc.vector.memset(tab_plane[:].bitcast(I32), 0)
+        nc.vector.memset(w2_plane[:].bitcast(I32), 0)
+        for q in range(4):
+            nc.gpsimd.dma_start(
+                tab_plane[32 * q : 32 * q + 4 * PASSES, :].bitcast(I32),
+                tab_scales[:, 4 * q : 4 * q + 4, :].bitcast(I32),
+            )
+        w2_codes = keep.tile([P, 2 * M], U8, name="w2_codes", align_bytes=64)
+        nc.gpsimd.dma_start(w2_codes[:].bitcast(I32), w2_words[0].bitcast(I32))
+        for q in range(4):
+            nc.gpsimd.dma_start(
+                w2_plane[32 * q : 32 * q + 4, :].bitcast(I32),
+                w2_scales[0, 4 * q : 4 * q + 4, :].bitcast(I32),
+            )
+        bias = keep.tile([P, N_TILES], F32, name="bias")
+        with nc.allow_non_contiguous_dma(reason="one bias value a partition"):
+            nc.gpsimd.dma_start(bias[:], b.rearrange("(c p) -> p c", p=P))
+
+        table = [keep.tile([P, T], U32, name="table%d" % a, align_bytes=64) for a in range(PASSES)]
+        w1_raw = [keep.tile([P, PACK, H], F32, name="w1_raw%d" % a) for a in range(PASSES)]
+        gates = [keep.tile([P, T], F32, name="gates%d" % n) for n in range(N_TILES)]
+
+        def load_table(a):
+            nc.sync.dma_start(table[a][:].bitcast(I32), tab_words[a].rearrange("p t i -> p (t i)").bitcast(I32))
+
+        def load_w1(a):
+            nc.sync.dma_start(w1_raw[a][:], w1[512 * a : 512 * (a + 1), :].rearrange("(p j) c -> p j c", j=PACK))
+
+        load_table(0)
+        load_w1(0)
+        load_w1(1)
+        load_table(1)
+        load_w1(2)
+        load_table(2)
+        for n in range(N_TILES):
+            nc.sync.dma_start(gates[n][:], gT[P * n : P * (n + 1), :])
+
+        picked = [keep.tile([P, S], U32, name="picked%d" % a, align_bytes=64) for a in range(PASSES)]
+        picked_plane = keep.tile([P, S], U8, name="picked_plane", align_bytes=64)
+        w1_bf = [keep.tile([P, PACK * H], BF16, name="w1_bf%d" % a, align_bytes=64) for a in range(PASSES)]
+        w1_codes = [keep.tile([P, H], U32, name="w1_codes%d" % a, align_bytes=64) for a in range(PASSES)]
+        w1_plane = [keep.tile([P, H], U8, name="w1_plane%d" % a, align_bytes=64) for a in range(PASSES)]
+        acc = [psum.tile([P, 512], F32, name="acc%d" % s, tag="bank%d" % s) for s in range(BANKS)]
+
+        def gather_words(a, j0, j1):
+            nc.vector.tensor_copy(picked[a][:, j0:j1], table[a][:].indirect(entries(j0, j1)))
+
+        def cast_views(a, m0, m1):
+            dst = w1_bf[a][:].rearrange("p (t m j) -> p m j t", t=PACK, j=PACK)[:, m0:m1]
+            src = w1_raw[a][:].rearrange("p j (m t) -> p m j t", t=PACK)[:, m0:m1]
+            return dst, src
+
+        def quantize_w1(a):
+            nc.vector.quantize_mx(out=w1_codes[a][:].bitcast(FP8X4), scales=w1_plane[a][:], in_=w1_bf[a][:])
+
+        def first_product(a, s):
+            cols = slice(P * s, P * (s + 1))
+            for t in range(PACK):
+                r_cols = slice(P * t, P * (t + 1))
+                nc.tensor.matmul_mx(
+                    out=acc[s][:, r_cols],
+                    lhsT=w1_codes[a][:, r_cols].bitcast(FP8X4),
+                    lhsT_scale=w1_plane[a][:, r_cols],
+                    rhs=picked[a][:, cols].bitcast(FP8X4),
+                    rhs_scale=picked_plane[4 * a : P, cols],
+                    start=(a == 0 and t == 0),
+                    stop=(a == PASSES - 1 and t == PACK - 1),
+                )
+
+        gather_words(0, 0, S)
+        nc.vector.tensor_copy(picked_plane[:], tab_plane[:].indirect(offsets[:]))
+        nc.scalar.copy(*cast_views(0, 0, P))
+        quantize_w1(0)
+        for s in range(BANKS):
+            first_product(0, s)
+        nc.scalar.copy(*cast_views(1, 0, P))
+        gather_words(1, 0, HALF)
+        quantize_w1(1)
+        gather_words(1, HALF, S)
+        for s in range(BANKS):
+            first_product(1, s)
+        nc.scalar.copy(*cast_views(2, 0, P // 2))
+        nc.vector.tensor_copy(*cast_views(2, P // 2, P))
+        quantize_w1(2)
+
+        h_bf = [keep.tile([P, PACK * HALF], BF16, name="h_bf%d" % u, align_bytes=64) for u in range(2)]
+        h_codes = [keep.tile([P, HALF], U32, name="h_codes%d" % u, align_bytes=64) for u in range(2)]
+        h_plane = [keep.tile([P, HALF], U8, name="h_plane%d" % u, align_bytes=64) for u in range(2)]
+
+        def relu(s):
+            u, i = divmod(s, 4)
+            dst = h_bf[u][:, 512 * i : 512 * (i + 1)].rearrange("p (s t) -> p s t", t=PACK)
+            nc.scalar.activation(dst, acc[s][:].rearrange("p (t s) -> p s t", t=PACK), ACT.Relu)
+
+        for quarter in range(4):
+            gather_words(2, 256 * quarter, 256 * (quarter + 1))
+            for s in (2 * quarter, 2 * quarter + 1):
+                first_product(2, s)
+        for s in range(6):
+            relu(s)
+
+        gate0 = keep.tile([P, S], F32, name="gate0")
+        for u in range(2):
+            nc.vector.tensor_copy(gate0[:, HALF * u : HALF * (u + 1)], gates[0][:].indirect(entries(HALF * u, HALF * (u + 1))))
+
+        y = {}
+
+        def second_product(u):
+            nc.vector.quantize_mx(out=h_codes[u][:].bitcast(FP8X4), scales=h_plane[u][:], in_=h_bf[u][:])
+            for n in range(N_TILES):
+                y[n, u] = psum.tile([P, HALF], F32, name="y%d_%d" % (n, u), tag="bank%d" % (4 * u + n))
+                nc.tensor.matmul_mx(
+                    out=y[n, u][:],
+                    lhsT=w2_codes[:, 2 * P * n : 2 * P * (n + 1)].bitcast(FP4X4),
+                    lhsT_scale=w2_plane[:, P * n : P * (n + 1)],
+                    rhs=h_codes[u][:].bitcast(FP8X4),
+                    rhs_scale=h_plane[u][:],
+                    start=True,
+                    stop=True,
+                )
+
+        def finish(n, u):
+            cols = slice(HALF * u, HALF * (u + 1))
+            act = keep.tile([P, HALF], F32, name="act%d_%d" % (n, u))
+            res = keep.tile([P, HALF], F32, name="res%d_%d" % (n, u))
+            nc.scalar.activation(act[:], y[n, u][:], ACT.Silu, bias=bias[:, n : n + 1])
+            if n == 0:
+                nc.vector.tensor_tensor(res[:], gate0[:, cols], act[:], MULT)
+            else:
+                nc.vector.tensor_tensor(res[:], gates[n][:].indirect(entries(HALF * u, HALF * (u + 1))), act[:], MULT)
+            nc.sync.dma_start(out[P * n : P * (n + 1), cols], res[:])
+
+        second_product(0)
+        finish(0, 0)
+        finish(1, 0)
+        relu(6)
+        relu(7)
+        second_product(1)
+        finish(2, 0)
+        finish(0, 1)
+        finish(1, 1)
+        finish(2, 1)
+        finish(3, 0)
+        finish(3, 1)

@@ -38,30 +38,14 @@ def tile_list_tabgate_silu_kernel(
         offsets = keep.tile([P, S // 16], U16, name="offsets")
         nc.sync.dma_start(offsets[:], offs)
 
-        warm = keep.tile([P, 8], F32, name="warm")
-        warm_out = keep.tile([P, 8], F32, name="warm_out")
-        nc.vector.memset(warm[:], 0.0)
-        nc.scalar.activation(warm_out[:], warm[:], ACT.Silu)
-
         tab_plane = keep.tile([P, T], U8, name="tab_plane", align_bytes=64)
         w2_plane = keep.tile([P, M], U8, name="w2_plane", align_bytes=64)
         nc.vector.memset(tab_plane[:].bitcast(I32), 0)
         nc.vector.memset(w2_plane[:].bitcast(I32), 0)
-        for q in range(4):
-            nc.gpsimd.dma_start(
-                tab_plane[32 * q : 32 * q + 4 * PASSES, :].bitcast(I32),
-                tab_scales[:, 4 * q : 4 * q + 4, :].bitcast(I32),
-            )
         w2_codes = keep.tile([P, 2 * M], U8, name="w2_codes", align_bytes=64)
-        nc.gpsimd.dma_start(w2_codes[:].bitcast(I32), w2_words[0].bitcast(I32))
-        for q in range(4):
-            nc.gpsimd.dma_start(
-                w2_plane[32 * q : 32 * q + 4, :].bitcast(I32),
-                w2_scales[0, 4 * q : 4 * q + 4, :].bitcast(I32),
-            )
-        bias = keep.tile([P, N_TILES], F32, name="bias")
-        with nc.allow_non_contiguous_dma(reason="one bias value a partition"):
-            nc.gpsimd.dma_start(bias[:], b.rearrange("(c p) -> p c", p=P))
+        bias_rows = keep.tile([P, P], F32, name="bias_rows", align_bytes=64)
+        bias = keep.tile([P, P], F32, name="bias", align_bytes=64)
+        nc.vector.memset(bias_rows[:], 0.0)
 
         table = [keep.tile([P, T], U32, name="table%d" % a, align_bytes=64) for a in range(PASSES)]
         w1_raw = [keep.tile([P, PACK, H], F32, name="w1_raw%d" % a) for a in range(PASSES)]
@@ -73,14 +57,36 @@ def tile_list_tabgate_silu_kernel(
         def load_w1(a):
             nc.sync.dma_start(w1_raw[a][:], w1[512 * a : 512 * (a + 1), :].rearrange("(p j) c -> p j c", j=PACK))
 
+        def load_gates(n):
+            nc.sync.dma_start(gates[n][:], gT[P * n : P * (n + 1), :])
+
         load_table(0)
+        for q in range(4):
+            nc.scalar.dma_start(
+                tab_plane[32 * q : 32 * q + 4 * PASSES, :].bitcast(I32),
+                tab_scales[:, 4 * q : 4 * q + 4, :].bitcast(I32),
+            )
+        warm = keep.tile([P, 8], F32, name="warm")
+        nc.scalar.activation(warm[:], bias_rows[:, 0:8], ACT.Silu)
         load_w1(0)
         load_w1(1)
         load_table(1)
         load_w1(2)
         load_table(2)
-        for n in range(N_TILES):
-            nc.sync.dma_start(gates[n][:], gT[P * n : P * (n + 1), :])
+        load_gates(0)
+        nc.sync.dma_start(w2_codes[:].bitcast(I32), w2_words[0].bitcast(I32))
+        for q in range(4):
+            nc.sync.dma_start(
+                w2_plane[32 * q : 32 * q + 4, :].bitcast(I32),
+                w2_scales[0, 4 * q : 4 * q + 4, :].bitcast(I32),
+            )
+        nc.sync.dma_start(
+            bias_rows[0:P:32, :].rearrange("q (c i) -> q c i", c=N_TILES),
+            b.rearrange("(c q i) -> q c i", c=N_TILES, q=4),
+        )
+        nc.vector.transpose(bias[:], bias_rows[:])
+        for n in range(1, N_TILES):
+            load_gates(n)
 
         picked = [keep.tile([P, S], U32, name="picked%d" % a, align_bytes=64) for a in range(PASSES)]
         picked_plane = keep.tile([P, S], U8, name="picked_plane", align_bytes=64)
@@ -120,9 +126,10 @@ def tile_list_tabgate_silu_kernel(
         quantize_w1(0)
         for s in range(BANKS):
             first_product(0, s)
-        nc.scalar.copy(*cast_views(1, 0, P))
-        gather_words(1, 0, HALF)
+        nc.scalar.copy(*cast_views(1, 0, P // 2))
+        nc.vector.tensor_copy(*cast_views(1, P // 2, P))
         quantize_w1(1)
+        gather_words(1, 0, HALF)
         gather_words(1, HALF, S)
         for s in range(BANKS):
             first_product(1, s)
@@ -130,7 +137,7 @@ def tile_list_tabgate_silu_kernel(
         nc.vector.tensor_copy(*cast_views(2, P // 2, P))
         quantize_w1(2)
 
-        h_bf = [keep.tile([P, PACK * HALF], BF16, name="h_bf%d" % u, align_bytes=64) for u in range(2)]
+        h_bf = [keep.tile([P, PACK * HALF], BF16, name="h_bf%d" % u, tag="h_bf%d" % u, align_bytes=64) for u in range(2)]
         h_codes = [keep.tile([P, HALF], U32, name="h_codes%d" % u, align_bytes=64) for u in range(2)]
         h_plane = [keep.tile([P, HALF], U8, name="h_plane%d" % u, align_bytes=64) for u in range(2)]
 
@@ -146,9 +153,11 @@ def tile_list_tabgate_silu_kernel(
         for s in range(6):
             relu(s)
 
-        gate0 = keep.tile([P, S], F32, name="gate0")
-        for u in range(2):
-            nc.vector.tensor_copy(gate0[:, HALF * u : HALF * (u + 1)], gates[0][:].indirect(entries(HALF * u, HALF * (u + 1))))
+        gate0 = {}
+
+        def gather_gate0(u, tag):
+            gate0[u] = keep.tile([P, HALF], F32, name="gate0_%d" % u, tag=tag, align_bytes=64)
+            nc.vector.tensor_copy(gate0[u][:], gates[0][:].indirect(entries(HALF * u, HALF * (u + 1))))
 
         y = {}
 
@@ -170,22 +179,20 @@ def tile_list_tabgate_silu_kernel(
             cols = slice(HALF * u, HALF * (u + 1))
             act = keep.tile([P, HALF], F32, name="act%d_%d" % (n, u))
             res = keep.tile([P, HALF], F32, name="res%d_%d" % (n, u))
-            nc.scalar.activation(act[:], y[n, u][:], ACT.Silu, bias=bias[:, n : n + 1])
+            nc.scalar.activation(act[:], y[n, u][:], ACT.Silu, bias=bias[:, 32 * n : 32 * n + 1])
             if n == 0:
-                nc.vector.tensor_tensor(res[:], gate0[:, cols], act[:], MULT)
+                nc.vector.tensor_tensor(res[:], gate0[u][:], act[:], MULT)
             else:
                 nc.vector.tensor_tensor(res[:], gates[n][:].indirect(entries(HALF * u, HALF * (u + 1))), act[:], MULT)
             nc.sync.dma_start(out[P * n : P * (n + 1), cols], res[:])
 
+        gather_gate0(0, "gate0")
         second_product(0)
+        gather_gate0(1, "h_bf0")
         finish(0, 0)
         finish(1, 0)
         relu(6)
         relu(7)
         second_product(1)
-        finish(2, 0)
-        finish(0, 1)
-        finish(1, 1)
-        finish(2, 1)
-        finish(3, 0)
-        finish(3, 1)
+        for n, u in ((2, 0), (0, 1), (1, 1), (2, 1), (3, 0), (3, 1)):
+            finish(n, u)

@@ -62,7 +62,7 @@ def tile_list_tabgate_silu_kernel(
 
         load_table(0)
         for q in range(4):
-            nc.scalar.dma_start(
+            (nc.sync if q < 2 else nc.scalar).dma_start(
                 tab_plane[32 * q : 32 * q + 4 * PASSES, :].bitcast(I32),
                 tab_scales[:, 4 * q : 4 * q + 4, :].bitcast(I32),
             )
@@ -70,11 +70,6 @@ def tile_list_tabgate_silu_kernel(
         nc.scalar.activation(warm[:], bias_rows[:, 0:8], ACT.Silu)
         load_w1(0)
         load_w1(1)
-        load_table(1)
-        load_w1(2)
-        load_table(2)
-        load_gates(0)
-        nc.sync.dma_start(w2_codes[:].bitcast(I32), w2_words[0].bitcast(I32))
         for q in range(4):
             nc.sync.dma_start(
                 w2_plane[32 * q : 32 * q + 4, :].bitcast(I32),
@@ -85,6 +80,11 @@ def tile_list_tabgate_silu_kernel(
             b.rearrange("(c q i) -> q c i", c=N_TILES, q=4),
         )
         nc.vector.transpose(bias[:], bias_rows[:])
+        load_table(1)
+        load_w1(2)
+        load_table(2)
+        load_gates(0)
+        nc.sync.dma_start(w2_codes[:].bitcast(I32), w2_words[0].bitcast(I32))
         for n in range(1, N_TILES):
             load_gates(n)
 
@@ -175,16 +175,17 @@ def tile_list_tabgate_silu_kernel(
                     stop=True,
                 )
 
-        def finish(n, u):
-            cols = slice(HALF * u, HALF * (u + 1))
+        def finish(n, u, pieces=1):
             act = keep.tile([P, HALF], F32, name="act%d_%d" % (n, u))
             res = keep.tile([P, HALF], F32, name="res%d_%d" % (n, u))
             nc.scalar.activation(act[:], y[n, u][:], ACT.Silu, bias=bias[:, 32 * n : 32 * n + 1])
-            if n == 0:
-                nc.vector.tensor_tensor(res[:], gate0[u][:], act[:], MULT)
-            else:
-                nc.vector.tensor_tensor(res[:], gates[n][:].indirect(entries(HALF * u, HALF * (u + 1))), act[:], MULT)
-            nc.sync.dma_start(out[P * n : P * (n + 1), cols], res[:])
+            width = HALF // pieces
+            for c0 in range(0, HALF, width):
+                cols = slice(c0, c0 + width)
+                j0 = HALF * u + c0
+                gate = gate0[u][:, cols] if n == 0 else gates[n][:].indirect(entries(j0, j0 + width))
+                nc.vector.tensor_tensor(res[:, cols], gate, act[:, cols], MULT)
+                nc.sync.dma_start(out[P * n : P * (n + 1), j0 : j0 + width], res[:, cols])
 
         gather_gate0(0, "gate0")
         second_product(0)
@@ -194,5 +195,6 @@ def tile_list_tabgate_silu_kernel(
         relu(6)
         relu(7)
         second_product(1)
-        for n, u in ((2, 0), (0, 1), (1, 1), (2, 1), (3, 0), (3, 1)):
+        for n, u in ((2, 0), (0, 1), (1, 1), (2, 1), (3, 0)):
             finish(n, u)
+        finish(3, 1, pieces=2)

from contextlib import ExitStack

import concourse.mybir as mybir

K, M, T, S, H = 1536, 512, 2048, 1024, 512
FLOPS = 2 * K * H * S + 2 * H * M * S

F32 = mybir.dt.float32
BF16 = mybir.dt.bfloat16
I32 = mybir.dt.int32
U32 = mybir.dt.uint32
U16 = mybir.dt.uint16
U8 = mybir.dt.uint8
FP8X4 = mybir.dt.float8_e4m3fn_x4
FP4X4 = mybir.dt.float4_e2m1fn_x4
ACT = mybir.ActivationFunctionType
MULT = mybir.AluOpType.mult

P = 128
PACK = 4
PASSES = K // (P * PACK)
BANKS = 8
HALF = S // 2
N_TILES = M // P


def tile_list_tabgate_silu_kernel(
    tc, tab_words, tab_scales, w1, w2_words, w2_scales, gT, b, offs, out
):
    nc = tc.nc
    with ExitStack() as ctx:
        keep = ctx.enter_context(tc.tile_pool(name="keep", bufs=1))
        psum = ctx.enter_context(tc.psum_pool(name="psum", bufs=1))

        def entries(j0, j1):
            return offsets[:, j0 // 16 : j1 // 16]

        offsets = keep.tile([P, S // 16], U16, name="offsets")
        nc.sync.dma_start(offsets[:], offs)

        tab_plane = keep.tile([P, T], U8, name="tab_plane", align_bytes=64)
        w2_plane = keep.tile([P, M], U8, name="w2_plane", align_bytes=64)
        nc.vector.memset(tab_plane[:].bitcast(I32), 0)
        nc.vector.memset(w2_plane[:].bitcast(I32), 0)
        w2_codes = keep.tile([P, 2 * M], U8, name="w2_codes", align_bytes=64)
        bias_rows = keep.tile([P, P], F32, name="bias_rows", align_bytes=64)
        bias = keep.tile([P, P], F32, name="bias", align_bytes=64)
        nc.vector.memset(bias_rows[:], 0.0)

        table = [keep.tile([P, T], U32, name="table%d" % a, align_bytes=64) for a in range(PASSES)]
        w1_raw = [keep.tile([P, PACK, H], F32, name="w1_raw%d" % a) for a in range(PASSES)]
        gates = [keep.tile([P, T], F32, name="gates%d" % n) for n in range(N_TILES)]

        def load_table(a):
            nc.sync.dma_start(table[a][:].bitcast(I32), tab_words[a].rearrange("p t i -> p (t i)").bitcast(I32))

        def load_w1(a):
            nc.sync.dma_start(w1_raw[a][:], w1[512 * a : 512 * (a + 1), :].rearrange("(p j) c -> p j c", j=PACK))

        def load_gates(n):
            nc.sync.dma_start(gates[n][:], gT[P * n : P * (n + 1), :])

        load_table(0)
        for q in range(4):
            (nc.sync if q < 2 else nc.scalar).dma_start(
                tab_plane[32 * q : 32 * q + 4 * PASSES, :].bitcast(I32),
                tab_scales[:, 4 * q : 4 * q + 4, :].bitcast(I32),
            )
        warm = keep.tile([P, 8], F32, name="warm")
        nc.scalar.activation(warm[:], bias_rows[:, 0:8], ACT.Silu)
        load_w1(0)
        load_w1(1)
        for q in range(4):
            nc.sync.dma_start(
                w2_plane[32 * q : 32 * q + 4, :].bitcast(I32),
                w2_scales[0, 4 * q : 4 * q + 4, :].bitcast(I32),
            )
        nc.sync.dma_start(
            bias_rows[0:P:32, :].rearrange("q (c i) -> q c i", c=N_TILES),
            b.rearrange("(c q i) -> q c i", c=N_TILES, q=4),
        )
        nc.vector.transpose(bias[:], bias_rows[:])
        load_table(1)
        load_w1(2)
        load_table(2)
        load_gates(0)
        nc.sync.dma_start(w2_codes[:].bitcast(I32), w2_words[0].bitcast(I32))
        for n in range(1, N_TILES):
            load_gates(n)

        picked = [keep.tile([P, S], U32, name="picked%d" % a, align_bytes=64) for a in range(PASSES)]
        picked_plane = keep.tile([P, S], U8, name="picked_plane", align_bytes=64)
        w1_bf = [keep.tile([P, PACK * H], BF16, name="w1_bf%d" % a, align_bytes=64) for a in range(PASSES)]
        w1_codes = [keep.tile([P, H], U32, name="w1_codes%d" % a, align_bytes=64) for a in range(PASSES)]
        w1_plane = [keep.tile([P, H], U8, name="w1_plane%d" % a, align_bytes=64) for a in range(PASSES)]
        acc = [psum.tile([P, 512], F32, name="acc%d" % s, tag="bank%d" % s) for s in range(BANKS)]

        def gather_words(a, j0, j1):
            nc.vector.tensor_copy(picked[a][:, j0:j1], table[a][:].indirect(entries(j0, j1)))

        def cast_views(a, m0, m1):
            dst = w1_bf[a][:].rearrange("p (t m j) -> p m j t", t=PACK, j=PACK)[:, m0:m1]
            src = w1_raw[a][:].rearrange("p j (m t) -> p m j t", t=PACK)[:, m0:m1]
            return dst, src

        def quantize_w1(a):
            nc.vector.quantize_mx(out=w1_codes[a][:].bitcast(FP8X4), scales=w1_plane[a][:], in_=w1_bf[a][:])

        def first_product(a, s):
            cols = slice(P * s, P * (s + 1))
            for t in range(PACK):
                r_cols = slice(P * t, P * (t + 1))
                nc.tensor.matmul_mx(
                    out=acc[s][:, r_cols],
                    lhsT=w1_codes[a][:, r_cols].bitcast(FP8X4),
                    lhsT_scale=w1_plane[a][:, r_cols],
                    rhs=picked[a][:, cols].bitcast(FP8X4),
                    rhs_scale=picked_plane[4 * a : P, cols],
                    start=(a == 0 and t == 0),
                    stop=(a == PASSES - 1 and t == PACK - 1),
                )

        gather_words(0, 0, S)
        nc.vector.tensor_copy(picked_plane[:], tab_plane[:].indirect(offsets[:]))
        nc.scalar.copy(*cast_views(0, 0, P))
        quantize_w1(0)
        for s in range(BANKS):
            first_product(0, s)
        nc.scalar.copy(*cast_views(1, 0, P // 2))
        nc.vector.tensor_copy(*cast_views(1, P // 2, P))
        quantize_w1(1)
        gather_words(1, 0, HALF)
        gather_words(1, HALF, S)
        for s in range(BANKS):
            first_product(1, s)
        nc.scalar.copy(*cast_views(2, 0, P // 2))
        nc.vector.tensor_copy(*cast_views(2, P // 2, P))
        quantize_w1(2)

        h_bf = [keep.tile([P, PACK * HALF], BF16, name="h_bf%d" % u, tag="h_bf%d" % u, align_bytes=64) for u in range(2)]
        h_codes = [keep.tile([P, HALF], U32, name="h_codes%d" % u, align_bytes=64) for u in range(2)]
        h_plane = [keep.tile([P, HALF], U8, name="h_plane%d" % u, align_bytes=64) for u in range(2)]

        def relu(s):
            u, i = divmod(s, 4)
            dst = h_bf[u][:, 512 * i : 512 * (i + 1)].rearrange("p (s t) -> p s t", t=PACK)
            nc.scalar.activation(dst, acc[s][:].rearrange("p (t s) -> p s t", t=PACK), ACT.Relu)

        for quarter in range(4):
            gather_words(2, 256 * quarter, 256 * (quarter + 1))
            for s in (2 * quarter, 2 * quarter + 1):
                first_product(2, s)
        for s in range(6):
            relu(s)

        gate0 = {}

        def gather_gate0(u, tag):
            gate0[u] = keep.tile([P, HALF], F32, name="gate0_%d" % u, tag=tag, align_bytes=64)
            nc.vector.tensor_copy(gate0[u][:], gates[0][:].indirect(entries(HALF * u, HALF * (u + 1))))

        y = {}

        def second_product(u):
            nc.vector.quantize_mx(out=h_codes[u][:].bitcast(FP8X4), scales=h_plane[u][:], in_=h_bf[u][:])
            for n in range(N_TILES):
                y[n, u] = psum.tile([P, HALF], F32, name="y%d_%d" % (n, u), tag="bank%d" % (4 * u + n))
                nc.tensor.matmul_mx(
                    out=y[n, u][:],
                    lhsT=w2_codes[:, 2 * P * n : 2 * P * (n + 1)].bitcast(FP4X4),
                    lhsT_scale=w2_plane[:, P * n : P * (n + 1)],
                    rhs=h_codes[u][:].bitcast(FP8X4),
                    rhs_scale=h_plane[u][:],
                    start=True,
                    stop=True,
                )

        def finish(n, u, pieces=1):
            act = keep.tile([P, HALF], F32, name="act%d_%d" % (n, u))
            res = keep.tile([P, HALF], F32, name="res%d_%d" % (n, u))
            nc.scalar.activation(act[:], y[n, u][:], ACT.Silu, bias=bias[:, 32 * n : 32 * n + 1])
            width = HALF // pieces
            for c0 in range(0, HALF, width):
                cols = slice(c0, c0 + width)
                j0 = HALF * u + c0
                gate = gate0[u][:, cols] if n == 0 else gates[n][:].indirect(entries(j0, j0 + width))
                nc.vector.tensor_tensor(res[:, cols], gate, act[:, cols], MULT)
                nc.sync.dma_start(out[P * n : P * (n + 1), j0 : j0 + width], res[:, cols])

        gather_gate0(0, "gate0")
        second_product(0)
        gather_gate0(1, "h_bf0")
        finish(0, 0)
        finish(1, 0)
        relu(6)
        relu(7)
        second_product(1)
        for n, u in ((2, 0), (0, 1), (1, 1), (2, 1), (3, 0)):
            finish(n, u)
        finish(3, 1, pieces=2)
